import numpy as np
import ml_dtypes


def mxq(x, axis, fmt="e4m3"):
    dtype, down = {"e4m3": (ml_dtypes.float8_e4m3fn, 7), "e5m2": (ml_dtypes.float8_e5m2, 14)}[fmt]
    v = np.moveaxis(np.asarray(x, np.float32).astype(ml_dtypes.bfloat16).astype(np.float64), axis, -1)
    blocks = v.reshape(v.shape[:-1] + (-1, 32))
    amax = np.abs(blocks).max(-1, keepdims=True)
    byte = np.maximum(np.where(amax > 0, np.frexp(amax)[1] - 1 + 127, 0) - down, 1)
    scale = np.exp2(byte - 127.0)
    codes = (blocks / scale).astype(np.float32).astype(dtype).astype(np.float64)
    return np.moveaxis((codes * scale).reshape(v.shape), -1, axis)


WIDE = False


def mx_kscale(k):
    if not WIDE:
        return np.ones(k)
    levels = np.array([10, -10, 5, -5, 0])
    if k % 512:
        return np.exp2(np.random.permutation(np.resize(levels, k // 32))).repeat(32)
    a = np.empty((k // 512, 16))
    for p in range(k // 512):
        a[p, :8] = np.random.permutation(np.resize(levels, 8))
        for g in range(8):
            far = levels[np.abs(levels - a[p, g]) >= 10]
            a[p, g + 8] = far[np.random.randint(len(far))]
    return np.exp2(a.ravel()).repeat(32)


def f64(x):
    return np.asarray(x).astype(np.float64)


def striped(idx):
    return np.tile(np.asarray(idx).reshape(-1, 16).T, (8, 1)).astype(np.uint16)


def unstriped(offs):
    return offs[:16].T.reshape(-1).astype(np.int64)


O, G, T, D, M = 9, 512, 2048, 512, 128


def setup_inputs():
    n = np.random.standard_normal
    s = mx_kscale(D)[:, None]
    x = n((D, T)) * s
    x[:, 0] = 0.0
    idx = np.stack([np.random.permutation(T - 1)[:G] + 1 for o in range(O)])
    idx[np.random.uniform(size=(O, G)) < 0.1] = 0
    return {
        "xT": x.astype(np.float32),
        "w": (n((O, D, M)) / np.sqrt(O * D) / s).astype(np.float32),
        "offs": striped(idx.reshape(-1)),
    }


def reference(xT, w, offs):
    x = f64(xT)[:, unstriped(offs)]
    wq, xq = mxq(f64(w), 1, "e4m3"), mxq(x, 0, "e4m3").reshape(D, O, G)
    y = sum(wq[o].T @ xq[:, o] for o in range(O))
    return y

@@ -1,0 +1,140 @@
+from contextlib import ExitStack
+
+import concourse.mybir as mybir
+
+TAPS, SITES, POOL, D, M = 9, 512, 2048, 512, 128
+FLOPS = 2 * M * SITES * TAPS * D
+
+F32 = mybir.dt.float32
+BF16 = mybir.dt.bfloat16
+U32 = mybir.dt.uint32
+U16 = mybir.dt.uint16
+U8 = mybir.dt.uint8
+FP8X4 = mybir.dt.float8_e4m3fn_x4
+COPY = mybir.ActivationFunctionType.Copy
+
+P = 128
+PACK = 4
+X_CHUNKS = (((0, 512), (512, 1024), (1024, 1536), (1536, 1792), (1792, 2048)), ((0, 1024), (1024, 2048)))
+PARTS = ((0, 256), (256, 384), (384, 512))
+WGROUPS = ((0, 4), (4, 8), (8, 9))
+W_QUANTIZE = ((0, 8), (8, 9))
+
+
+def tile_attend_spconv_kernel(tc, xT, w, offs, out):
+    nc = tc.nc
+    x_rows = xT.rearrange("(p j) c -> p j c", j=PACK)
+    w_rows = w.rearrange("o (p j) m -> p o (j m)", j=PACK)
+
+    with ExitStack() as ctx:
+        held = ctx.enter_context(tc.tile_pool(name="held", bufs=1))
+        psum = ctx.enter_context(tc.psum_pool(name="psum", bufs=1))
+
+        offsets = held.tile([P, TAPS * SITES // 16], U16, name="offsets")
+        raw = [[held.tile([P, 2, b - a], F32, name=f"raw{u}_{a}") for a, b in X_CHUNKS[u]] for u in range(2)]
+        table = [held.tile([P, POOL * 2], BF16, name=f"table{u}", align_bytes=64) for u in range(2)]
+        w_raw = [held.tile([P, b - a, PACK * M], F32, name=f"w_raw{a}") for a, b in WGROUPS]
+        w_grouped = held.tile([P, TAPS * M * PACK], BF16, name="w_grouped", align_bytes=64)
+        w_codes = held.tile([P, TAPS * M], U32, name="w_codes", align_bytes=64)
+        w_scales = held.tile([P, TAPS * M], U8, name="w_scales", align_bytes=64)
+        picked = [held.tile([P, 2, SITES * 2], BF16, name=f"picked{o}", align_bytes=64) for o in range(TAPS)]
+        grouped = [held.tile([P, SITES * PACK], BF16, name=f"grouped{o}", align_bytes=64) for o in range(TAPS)]
+        codes = [held.tile([P, SITES], U32, name=f"codes{o}", align_bytes=64) for o in range(TAPS)]
+        scales = [held.tile([P, SITES], U8, name=f"scales{o}", align_bytes=64) for o in range(TAPS)]
+        acc = [psum.tile([M, b - a], F32, name=f"acc{a}") for a, b in PARTS]
+        result = [held.tile([M, b - a], F32, name=f"result{a}") for a, b in PARTS]
+
+        for u in range(2):
+            for k, (a, b) in enumerate(X_CHUNKS[u]):
+                nc.sync.dma_start(out=raw[u][k][:], in_=x_rows[:, 2 * u : 2 * u + 2, a:b])
+            if u == 0:
+                nc.sync.dma_start(offsets[:], offs)
+        for g, (a, b) in enumerate(WGROUPS):
+            nc.sync.dma_start(out=w_raw[g][:], in_=w_rows[:, a:b, :])
+
+        def cast(engine, u, k, a, b):
+            c0 = X_CHUNKS[u][k][0]
+            dst = table[u][:, 2 * (c0 + a) : 2 * (c0 + b)].rearrange("p (c e) -> p c e", e=2)
+            src = raw[u][k][:, :, a:b].rearrange("p e c -> p c e")
+            if engine == 0:
+                nc.vector.tensor_copy(dst, src)
+            else:
+                nc.scalar.activation(dst, src, COPY)
+
+        def gather(u, o, a, b):
+            list_columns = offsets[:, (o * SITES + a) // 16 : (o * SITES + b) // 16]
+            nc.vector.tensor_copy(picked[o][:, u, 2 * a : 2 * b].bitcast(U32), table[u][:].bitcast(U32).indirect(list_columns))
+
+        def interleave(o, a, b):
+            nc.scalar.copy(
+                grouped[o][:, PACK * a : PACK * b].bitcast(F32).rearrange("p (c u) -> p c u", u=2),
+                picked[o][:, :, 2 * a : 2 * b].bitcast(F32).rearrange("p u c -> p c u"),
+            )
+
+        def quantize(o, a, b):
+            nc.vector.quantize_mx(out=codes[o][:, a:b].bitcast(FP8X4), scales=scales[o][:, a:b], in_=grouped[o][:, PACK * a : PACK * b])
+
+        def multiply(o, h):
+            cols = slice(*PARTS[h])
+            w_cols = slice(o * M, (o + 1) * M)
+            nc.tensor.matmul_mx(
+                out=acc[h][:],
+                lhsT=w_codes[:, w_cols].bitcast(FP8X4),
+                lhsT_scale=w_scales[:, w_cols],
+                rhs=codes[o][:, cols].bitcast(FP8X4),
+                rhs_scale=scales[o][:, cols],
+                start=(o == 0),
+                stop=(o == TAPS - 1),
+            )
+
+        for k, (a, b) in enumerate(X_CHUNKS[0]):
+            cut = (b - a) * 5 // 8
+            cast(0, 0, k, 0, cut)
+            cast(1, 0, k, cut, b - a)
+        for o in range(TAPS):
+            gather(0, o, 0, SITES)
+        for k, (a, b) in enumerate(X_CHUNKS[1]):
+            for c in range(0, b - a, 512):
+                cast(1, 1, k, c, c + 512)
+        for g, (a, b) in enumerate(WGROUPS):
+            for o in range(a, b):
+                nc.scalar.activation(
+                    w_grouped[:, o * M * PACK : (o + 1) * M * PACK].rearrange("p (m j) -> p m j", j=PACK),
+                    w_raw[g][:, o - a, :].rearrange("p (j m) -> p m j", j=PACK),
+                    COPY,
+                )
+
+        last = TAPS - 1
+        for o in range(last):
+            gather(1, o, 0, SITES)
+            interleave(o, 0, SITES)
+            if o == 1:
+                for a, b in W_QUANTIZE:
+                    nc.vector.quantize_mx(
+                        out=w_codes[:, a * M : b * M].bitcast(FP8X4),
+                        scales=w_scales[:, a * M : b * M],
+                        in_=w_grouped[:, a * M * PACK : b * M * PACK],
+                    )
+            if o >= 2:
+                quantize(o - 2, 0, SITES)
+                for h in range(len(PARTS)):
+                    multiply(o - 2, h)
+        gather(1, last, 0, 256)
+        interleave(last, 0, 256)
+        quantize(last - 2, 0, SITES)
+        gather(1, last, 256, SITES)
+        interleave(last, 256, SITES)
+        for h in range(len(PARTS)):
+            multiply(last - 2, h)
+        quantize(last - 1, 0, SITES)
+        for h in range(len(PARTS)):
+            multiply(last - 1, h)
+        for h in range(len(PARTS)):
+            quantize(last, *PARTS[h])
+            multiply(last, h)
+        for h, (a, b) in enumerate(PARTS):
+            if h < 2:
+                nc.scalar.copy(result[h][:], acc[h][:])
+            else:
+                nc.vector.tensor_copy(result[h][:], acc[h][:])
+            nc.sync.dma_start(out=out[:, a:b], in_=result[h][:])

@@ -15,7 +15,7 @@ COPY = mybir.ActivationFunctionType.Copy
 
 P = 128
 PACK = 4
-X_CHUNKS = (((0, 512), (512, 1024), (1024, 1536), (1536, 1792), (1792, 2048)), ((0, 1024), (1024, 2048)))
+X_CHUNKS = (((0, 1024), (1024, 1536), (1536, 1792), (1792, 2048)), ((0, 1024), (1024, 2048)))
 PARTS = ((0, 256), (256, 384), (384, 512))
 WGROUPS = ((0, 4), (4, 8), (8, 9))
 W_QUANTIZE = ((0, 8), (8, 9))
@@ -91,7 +91,8 @@ def tile_attend_spconv_kernel(tc, xT, w, offs, out):
             cut = (b - a) * 5 // 8
             cast(0, 0, k, 0, cut)
             cast(1, 0, k, cut, b - a)
-        for o in range(TAPS):
+        early = 5
+        for o in range(early):
             gather(0, o, 0, SITES)
         for k, (a, b) in enumerate(X_CHUNKS[1]):
             for c in range(0, b - a, 512):
@@ -104,34 +105,41 @@ def tile_attend_spconv_kernel(tc, xT, w, offs, out):
                     COPY,
                 )
 
-        last = TAPS - 1
-        for o in range(last):
-            gather(1, o, 0, SITES)
-            interleave(o, 0, SITES)
-            if o == 1:
-                for a, b in W_QUANTIZE:
-                    nc.vector.quantize_mx(
-                        out=w_codes[:, a * M : b * M].bitcast(FP8X4),
-                        scales=w_scales[:, a * M : b * M],
-                        in_=w_grouped[:, a * M * PACK : b * M * PACK],
-                    )
-            if o >= 2:
-                quantize(o - 2, 0, SITES)
-                for h in range(len(PARTS)):
-                    multiply(o - 2, h)
-        gather(1, last, 0, 256)
-        interleave(last, 0, 256)
-        quantize(last - 2, 0, SITES)
-        gather(1, last, 256, SITES)
-        interleave(last, 256, SITES)
-        for h in range(len(PARTS)):
-            multiply(last - 2, h)
-        quantize(last - 1, 0, SITES)
-        for h in range(len(PARTS)):
-            multiply(last - 1, h)
-        for h in range(len(PARTS)):
-            quantize(last, *PARTS[h])
-            multiply(last, h)
+        def second(o, a, b):
+            gather(1, o, a, b)
+            interleave(o, a, b)
+
+        def finish(o):
+            quantize(o, 0, SITES)
+            for h in range(len(PARTS)):
+                multiply(o, h)
+
+        for o in range(early, TAPS):
+            second(o - early, 0, SITES)
+            gather(0, o, 0, SITES)
+        second(4, 0, SITES)
+        for a, b in W_QUANTIZE:
+            nc.vector.quantize_mx(
+                out=w_codes[:, a * M : b * M].bitcast(FP8X4),
+                scales=w_scales[:, a * M : b * M],
+                in_=w_grouped[:, a * M * PACK : b * M * PACK],
+            )
+        finish(0)
+        second(5, 0, SITES)
+        finish(1)
+        finish(2)
+        second(6, 0, SITES)
+        finish(3)
+        second(7, 0, SITES)
+        finish(4)
+        second(8, 0, 256)
+        finish(5)
+        finish(6)
+        second(8, 256, SITES)
+        finish(7)
+        for h, (a, b) in enumerate(PARTS):
+            quantize(8, a, b)
+            multiply(8, h)
         for h, (a, b) in enumerate(PARTS):
             if h < 2:
                 nc.scalar.copy(result[h][:], acc[h][:])

from contextlib import ExitStack

import concourse.mybir as mybir

TAPS, SITES, POOL, D, M = 9, 512, 2048, 512, 128
FLOPS = 2 * M * SITES * TAPS * D

F32 = mybir.dt.float32
BF16 = mybir.dt.bfloat16
U32 = mybir.dt.uint32
U16 = mybir.dt.uint16
U8 = mybir.dt.uint8
FP8X4 = mybir.dt.float8_e4m3fn_x4
COPY = mybir.ActivationFunctionType.Copy

P = 128
PACK = 4
X_CHUNKS = (((0, 1024), (1024, 1536), (1536, 1792), (1792, 2048)), ((0, 1024), (1024, 2048)))
PARTS = ((0, 256), (256, 384), (384, 512))
WGROUPS = ((0, 4), (4, 8), (8, 9))
W_QUANTIZE = ((0, 8), (8, 9))


def tile_attend_spconv_kernel(tc, xT, w, offs, out):
    nc = tc.nc
    x_rows = xT.rearrange("(p j) c -> p j c", j=PACK)
    w_rows = w.rearrange("o (p j) m -> p o (j m)", j=PACK)

    with ExitStack() as ctx:
        held = ctx.enter_context(tc.tile_pool(name="held", bufs=1))
        psum = ctx.enter_context(tc.psum_pool(name="psum", bufs=1))

        offsets = held.tile([P, TAPS * SITES // 16], U16, name="offsets")
        raw = [[held.tile([P, 2, b - a], F32, name=f"raw{u}_{a}") for a, b in X_CHUNKS[u]] for u in range(2)]
        table = [held.tile([P, POOL * 2], BF16, name=f"table{u}", align_bytes=64) for u in range(2)]
        w_raw = [held.tile([P, b - a, PACK * M], F32, name=f"w_raw{a}") for a, b in WGROUPS]
        w_grouped = held.tile([P, TAPS * M * PACK], BF16, name="w_grouped", align_bytes=64)
        w_codes = held.tile([P, TAPS * M], U32, name="w_codes", align_bytes=64)
        w_scales = held.tile([P, TAPS * M], U8, name="w_scales", align_bytes=64)
        picked = [held.tile([P, 2, SITES * 2], BF16, name=f"picked{o}", align_bytes=64) for o in range(TAPS)]
        grouped = [held.tile([P, SITES * PACK], BF16, name=f"grouped{o}", align_bytes=64) for o in range(TAPS)]
        codes = [held.tile([P, SITES], U32, name=f"codes{o}", align_bytes=64) for o in range(TAPS)]
        scales = [held.tile([P, SITES], U8, name=f"scales{o}", align_bytes=64) for o in range(TAPS)]
        acc = [psum.tile([M, b - a], F32, name=f"acc{a}") for a, b in PARTS]
        result = [held.tile([M, b - a], F32, name=f"result{a}") for a, b in PARTS]

        for u in range(2):
            for k, (a, b) in enumerate(X_CHUNKS[u]):
                nc.sync.dma_start(out=raw[u][k][:], in_=x_rows[:, 2 * u : 2 * u + 2, a:b])
            if u == 0:
                nc.sync.dma_start(offsets[:], offs)
        for g, (a, b) in enumerate(WGROUPS):
            nc.sync.dma_start(out=w_raw[g][:], in_=w_rows[:, a:b, :])

        def cast(engine, u, k, a, b):
            c0 = X_CHUNKS[u][k][0]
            dst = table[u][:, 2 * (c0 + a) : 2 * (c0 + b)].rearrange("p (c e) -> p c e", e=2)
            src = raw[u][k][:, :, a:b].rearrange("p e c -> p c e")
            if engine == 0:
                nc.vector.tensor_copy(dst, src)
            else:
                nc.scalar.activation(dst, src, COPY)

        def gather(u, o, a, b):
            list_columns = offsets[:, (o * SITES + a) // 16 : (o * SITES + b) // 16]
            nc.vector.tensor_copy(picked[o][:, u, 2 * a : 2 * b].bitcast(U32), table[u][:].bitcast(U32).indirect(list_columns))

        def interleave(o, a, b):
            nc.scalar.copy(
                grouped[o][:, PACK * a : PACK * b].bitcast(F32).rearrange("p (c u) -> p c u", u=2),
                picked[o][:, :, 2 * a : 2 * b].bitcast(F32).rearrange("p u c -> p c u"),
            )

        def quantize(o, a, b):
            nc.vector.quantize_mx(out=codes[o][:, a:b].bitcast(FP8X4), scales=scales[o][:, a:b], in_=grouped[o][:, PACK * a : PACK * b])

        def multiply(o, h):
            cols = slice(*PARTS[h])
            w_cols = slice(o * M, (o + 1) * M)
            nc.tensor.matmul_mx(
                out=acc[h][:],
                lhsT=w_codes[:, w_cols].bitcast(FP8X4),
                lhsT_scale=w_scales[:, w_cols],
                rhs=codes[o][:, cols].bitcast(FP8X4),
                rhs_scale=scales[o][:, cols],
                start=(o == 0),
                stop=(o == TAPS - 1),
            )

        for k, (a, b) in enumerate(X_CHUNKS[0]):
            cut = (b - a) * 5 // 8
            cast(0, 0, k, 0, cut)
            cast(1, 0, k, cut, b - a)
        early = 5
        for o in range(early):
            gather(0, o, 0, SITES)
        for k, (a, b) in enumerate(X_CHUNKS[1]):
            for c in range(0, b - a, 512):
                cast(1, 1, k, c, c + 512)
        for g, (a, b) in enumerate(WGROUPS):
            for o in range(a, b):
                nc.scalar.activation(
                    w_grouped[:, o * M * PACK : (o + 1) * M * PACK].rearrange("p (m j) -> p m j", j=PACK),
                    w_raw[g][:, o - a, :].rearrange("p (j m) -> p m j", j=PACK),
                    COPY,
                )

        def second(o, a, b):
            gather(1, o, a, b)
            interleave(o, a, b)

        def finish(o):
            quantize(o, 0, SITES)
            for h in range(len(PARTS)):
                multiply(o, h)

        for o in range(early, TAPS):
            second(o - early, 0, SITES)
            gather(0, o, 0, SITES)
        second(4, 0, SITES)
        for a, b in W_QUANTIZE:
            nc.vector.quantize_mx(
                out=w_codes[:, a * M : b * M].bitcast(FP8X4),
                scales=w_scales[:, a * M : b * M],
                in_=w_grouped[:, a * M * PACK : b * M * PACK],
            )
        finish(0)
        second(5, 0, SITES)
        finish(1)
        finish(2)
        second(6, 0, SITES)
        finish(3)
        second(7, 0, SITES)
        finish(4)
        second(8, 0, 256)
        finish(5)
        finish(6)
        second(8, 256, SITES)
        finish(7)
        for h, (a, b) in enumerate(PARTS):
            quantize(8, a, b)
            multiply(8, h)
        for h, (a, b) in enumerate(PARTS):
            if h < 2:
                nc.scalar.copy(result[h][:], acc[h][:])
            else:
                nc.vector.tensor_copy(result[h][:], acc[h][:])
            nc.sync.dma_start(out=out[:, a:b], in_=result[h][:])
